import numpy as np
import ml_dtypes


def mxq(x, axis, fmt="e4m3"):
    dtype, down = {"e4m3": (ml_dtypes.float8_e4m3fn, 7), "e5m2": (ml_dtypes.float8_e5m2, 14)}[fmt]
    v = np.moveaxis(np.asarray(x, np.float32).astype(ml_dtypes.bfloat16).astype(np.float64), axis, -1)
    blocks = v.reshape(v.shape[:-1] + (-1, 32))
    amax = np.abs(blocks).max(-1, keepdims=True)
    byte = np.maximum(np.where(amax > 0, np.frexp(amax)[1] - 1 + 127, 0) - down, 1)
    scale = np.exp2(byte - 127.0)
    codes = (blocks / scale).astype(np.float32).astype(dtype).astype(np.float64)
    return np.moveaxis((codes * scale).reshape(v.shape), -1, axis)


WIDE = False


def mx_kscale(k):
    if not WIDE:
        return np.ones(k)
    levels = np.array([10, -10, 5, -5, 0])
    if k % 512:
        return np.exp2(np.random.permutation(np.resize(levels, k // 32))).repeat(32)
    a = np.empty((k // 512, 16))
    for p in range(k // 512):
        a[p, :8] = np.random.permutation(np.resize(levels, 8))
        for g in range(8):
            far = levels[np.abs(levels - a[p, g]) >= 10]
            a[p, g + 8] = far[np.random.randint(len(far))]
    return np.exp2(a.ravel()).repeat(32)


def f64(x):
    return np.asarray(x).astype(np.float64)


def striped(idx):
    return np.tile(np.asarray(idx).reshape(-1, 16).T, (8, 1)).astype(np.uint16)


def unstriped(offs):
    return offs[:16].T.reshape(-1).astype(np.int64)


def sigmoid(v):
    return 1.0 / (1.0 + np.exp(-v))


def bf(x):
    return np.asarray(x, np.float32).astype(ml_dtypes.bfloat16)


def planes(Y):
    r, m = Y.shape
    b = f64(bf(Y)).reshape(r // 32, 32, m)
    amax = np.abs(b).max(1)
    byte = np.clip(np.where(amax > 0, np.frexp(amax)[1] - 1 + 127 - 7, 1), 1, 254)
    codes = (b * np.exp2(127.0 - byte)[:, None, :]).reshape(r, m).astype(np.float32).astype(ml_dtypes.float8_e4m3fn).view(np.uint8)
    words = codes.reshape(r // 512, 128, 4, m).transpose(0, 1, 3, 2)
    return np.ascontiguousarray(words), np.ascontiguousarray(byte.astype(np.uint8).reshape(r // 512, 16, m))


D, T, I, Q, E, G = 512, 2048, 1024, 256, 512, 64


def setup_inputs():
    n = np.random.standard_normal
    idx = (np.random.permutation(T // 16)[:I // 16, None] * 16 + np.arange(16)).reshape(-1)
    fd = mx_kscale(D)
    fi = mx_kscale(I)
    ti = np.ones(T)
    ti[idx] = fi
    return {
        "query": (n((D, Q)) * 0.4 / np.sqrt(D) * fd[:, None]).astype(np.float32),
        "keys": (n((D, T)) / fd[:, None]).astype(np.float32),
        "th": (np.random.uniform(-0.5, 0.5, (Q, 1))).astype(np.float32),
        "size": (np.random.uniform(0.5, 2.0, (1, I)) * fi).astype(np.float32),
        "vals": (n((E, T)) / ti).astype(np.float32),
        "offs": striped(idx),
    }


def reference(query, keys, th, size, vals, offs):
    idx = unstriped(offs)
    kb = f64(keys)[:, idx].reshape(D, G, I // G).mean(axis=2)
    queryq = mxq(f64(query), 0, "e4m3")
    kbq = mxq(kb, 0, "e4m3")
    b = queryq.T @ kbq
    gate = sigmoid(4.0 * b - f64(th))
    gr = np.repeat(gate, I // G, axis=1)
    keysidxq = mxq(f64(keys)[:, idx], 0, "e4m3")
    a = queryq.T @ keysidxq
    p = np.exp(a - np.max(a, axis=1, keepdims=True)) * gr
    w = p * f64(size) / np.sum(p, axis=1, keepdims=True)
    wt = w.T
    vt = f64(vals)[:, idx].T
    vtq = mxq(vt, 0, "e4m3")
    wtq = mxq(wt, 0, "e4m3")
    o = vtq.T @ wtq
    words, scales = planes(o)
    return o, words, scales

@@ -1,0 +1,261 @@
+from contextlib import ExitStack
+
+import concourse.mybir as mybir
+from concourse.masks import make_identity
+
+D, T, I, Q, E, G = 512, 2048, 1024, 256, 512, 64
+FLOPS = 2 * D * Q * G + 2 * D * Q * I + 2 * I * E * Q
+
+F32 = mybir.dt.float32
+BF16 = mybir.dt.bfloat16
+I32 = mybir.dt.int32
+U32 = mybir.dt.uint32
+U16 = mybir.dt.uint16
+U8 = mybir.dt.uint8
+FP8X4 = mybir.dt.float8_e4m3fn_x4
+ALU = mybir.AluOpType
+ACT = mybir.ActivationFunctionType
+AXIS = mybir.AxisListType
+
+P = 128
+PACK = 4
+PASS = P * PACK
+BLOCK = I // G
+RUN = I // P
+QB = Q // P
+PASSES = I // PASS
+LIST_COLS = PASS // 16
+
+
+def tile_attend_moba_pl_kernel(tc, query, keys, th, size, vals, offs, out_0, out_1, out_2):
+    nc = tc.nc
+    with ExitStack() as ctx:
+        sb = ctx.enter_context(tc.tile_pool(name="sb", bufs=1))
+        ps = ctx.enter_context(tc.psum_pool(name="ps", bufs=1))
+
+        def sbuf(name, cols, dtype):
+            return sb.tile([P, cols], dtype, name=name, align_bytes=64)
+
+        def bank(tag, name):
+            return ps.tile([P, PASS], F32, name=name, tag=tag)
+
+        def quantize(codes, scales, values):
+            nc.vector.quantize_mx(out=codes.bitcast(FP8X4), scales=scales, in_=values)
+
+        def multiply(out, lhs, lhs_cols, rhs, rhs_cols, start, stop):
+            nc.tensor.matmul_mx(
+                out=out,
+                lhsT=lhs[0][:, lhs_cols].bitcast(FP8X4),
+                lhsT_scale=lhs[1][:, lhs_cols],
+                rhs=rhs[0][:, rhs_cols].bitcast(FP8X4),
+                rhs_scale=rhs[1][:, rhs_cols],
+                start=start,
+                stop=stop,
+            )
+
+        def mx_tiles(name, cols):
+            return sbuf(name + "_codes", cols, U32), sbuf(name + "_scales", cols, U8)
+
+        offsets = sb.tile([P, I // 16], U16, name="offsets")
+        nc.sync.dma_start(offsets[:], offs)
+        size_rows = sbuf("size_rows", RUN, F32)
+        nc.scalar.dma_start(size_rows[:], size.rearrange("o (n m) -> (o n) m", m=RUN))
+        th_cols = sbuf("th_cols", QB, F32)
+        with nc.allow_non_contiguous_dma(reason="one threshold a partition and query block"):
+            nc.scalar.dma_start(th_cols[:], th.rearrange("(b p) o -> p (b o)", p=P))
+        ident = sbuf("ident", P, F32)
+        make_identity(nc, ident[:])
+        key_rows = keys.rearrange("(p t) n -> p t n", t=PACK)
+        val_rows = vals.rearrange("(p t) n -> p t n", t=PACK)
+        key_pool = [sbuf("key_pool%d" % t, T, F32) for t in range(PACK)]
+        val_pool = [sbuf("val_pool%d" % t, T, F32) for t in range(PACK)]
+        for t in range(PACK):
+            nc.sync.dma_start(key_pool[t][:], key_rows[:, t, :])
+        query_raw = sbuf("query_raw", PACK * Q, F32)
+        nc.sync.dma_start(val_pool[0][:], val_rows[:, 0, :])
+        nc.sync.dma_start(query_raw[:], query.rearrange("(p t) q -> p (t q)", t=PACK))
+        for t in range(1, PACK):
+            nc.sync.dma_start(val_pool[t][:], val_rows[:, t, :])
+
+        size_all = sbuf("size_all", I, F32)
+        size_view = size_all[:].rearrange("p (n m) -> p n m", m=RUN)
+        for half in range(2):
+            spread = bank("score%d" % half, "spread%d" % half)
+            for m in range(PACK):
+                col = PACK * half + m
+                nc.tensor.transpose(spread[:, P * m : P * (m + 1)], size_rows[:, col : col + 1].to_broadcast([P, P]), ident[:])
+            nc.scalar.activation(
+                size_view[:, :, PACK * half : PACK * (half + 1)],
+                spread[:].rearrange("p (m n) -> p n m", m=PACK),
+                ACT.Copy,
+            )
+
+        def pass_offsets(h):
+            return offsets[:, LIST_COLS * h : LIST_COLS * (h + 1)]
+
+        picked = sbuf("picked", PACK * I, F32)
+        picked_view = picked[:].rearrange("p (t s) -> p s t", t=PACK)
+        key16 = sbuf("key16", PACK * I, BF16)
+        key16_view = key16[:].rearrange("p (s t) -> p s t", t=PACK)
+        key_mx = mx_tiles("key", I)
+        run_sums = bank("runs", "run_sums")
+        run_means = sbuf("run_means", PASS, F32)
+        back = bank("back", "back")
+
+        def sum_runs(t):
+            for j in range(RUN):
+                nc.tensor.matmul(
+                    run_sums[:, P * t : P * (t + 1)],
+                    picked[:, I * t + j : I * (t + 1) : RUN],
+                    ident[:],
+                    start=(j == 0),
+                    stop=(j == RUN - 1),
+                    is_transpose=True,
+                )
+
+        def turn_back(t0, t1):
+            nc.scalar.activation(run_means[:, P * t0 : P * t1], run_sums[:, P * t0 : P * t1], ACT.Copy, scale=1.0 / BLOCK)
+            for t in range(t0, t1):
+                nc.tensor.transpose(back[:, P * t : P * (t + 1)], run_means[:, P * t : P * (t + 1)], ident[:])
+
+        def round_keys(slots, u):
+            nc.scalar.copy(key16_view[:, slots, 2 * u : 2 * u + 2], picked_view[:, slots, 2 * u : 2 * u + 2])
+
+        last = PACK - 1
+        for t in range(last):
+            nc.vector.tensor_copy(picked[:, I * t : I * (t + 1)], key_pool[t][:].indirect(offsets[:]))
+            sum_runs(t)
+            if t == 1:
+                round_keys(slice(0, I), 0)
+        turn_back(0, last)
+        for h in range(PASSES):
+            slots = slice(PASS * h, PASS * (h + 1))
+            nc.vector.tensor_copy(picked[:, I * last + PASS * h : I * last + PASS * (h + 1)], key_pool[last][:].indirect(pass_offsets(h)))
+            round_keys(slots, 1)
+        sum_runs(last)
+        turn_back(last, PACK)
+
+        query16 = sbuf("query16", PACK * Q, BF16)
+        nc.scalar.copy(query16[:].rearrange("p (q t) -> p q t", t=PACK), query_raw[:].rearrange("p (t q) -> p q t", t=PACK))
+        query_mx = mx_tiles("query", Q)
+        quantize(query_mx[0][:], query_mx[1][:], query16[:])
+
+        negated = [sbuf("negated%d" % b, I, F32) for b in range(QB)]
+        least = [[sbuf("least%d_%d" % (b, h), 1, F32) for h in range(PASSES)] for b in range(QB)]
+        for h in range(PASSES):
+            slots = slice(PASS * h, PASS * (h + 1))
+            quantize(key_mx[0][:, slots], key_mx[1][:, slots], key16[:, PACK * PASS * h : PACK * PASS * (h + 1)])
+            for b in range(QB):
+                score = bank("score%d" % (QB * h + b), "score%d_%d" % (b, h))
+                multiply(score[:], query_mx, slice(P * b, P * (b + 1)), key_mx, slots, True, True)
+                nc.vector.tensor_scalar(
+                    negated[b][:, slots],
+                    score[:],
+                    -1.0,
+                    None if h == 0 else least[b][h - 1][:],
+                    ALU.mult,
+                    ALU.min,
+                    accum_out=least[b][h][:],
+                )
+
+        mean16 = sbuf("mean16", PACK * G, BF16)
+        with nc.allow_low_precision(reason="float32 sum, rounded once for the quantiser"):
+            nc.vector.tensor_reduce(
+                mean16[:].rearrange("p (g t) -> p g t", t=PACK),
+                back[:].rearrange("p (t g h) -> p g t h", t=PACK, h=2),
+                AXIS.X,
+                ALU.add,
+            )
+        mean_mx = mx_tiles("mean", G)
+        quantize(mean_mx[0][:], mean_mx[1][:], mean16[:])
+        block_score = bank("runs", "block_score")
+        above = sbuf("above", QB * G, F32)
+        dist = sbuf("dist", QB * G, F32)
+        for b in range(QB):
+            multiply(block_score[:, G * b : G * (b + 1)], query_mx, slice(P * b, P * (b + 1)), mean_mx, slice(0, G), True, True)
+        for b in range(QB):
+            cols = slice(G * b, G * (b + 1))
+            nc.scalar.activation(above[:, cols], block_score[:, cols], ACT.Relu, bias=th_cols[:, b : b + 1], scale=-4.0)
+            nc.scalar.activation(dist[:, cols], block_score[:, cols], ACT.Abs, bias=th_cols[:, b : b + 1], scale=-4.0)
+        fall = sbuf("fall", QB * G, F32)
+        rise = sbuf("rise", QB * G, F32)
+        nc.scalar.activation(fall[:], above[:], ACT.Exp, scale=-1.0)
+        nc.scalar.activation(rise[:], dist[:], ACT.Tanh, scale=0.5)
+        gate = sbuf("gate", QB * G, F32)
+        nc.vector.scalar_tensor_tensor(gate[:], rise[:], 1.0, fall[:], ALU.add, ALU.mult)
+
+        def turn(values16, tag, name):
+            words = values16[:].bitcast(F32)
+            turned = bank(tag, name + "_turned")
+            for h in range(PASSES):
+                for u in range(2):
+                    c = 2 * h + u
+                    nc.tensor.transpose(turned[:, P * c : P * (c + 1)], words[:, 2 * P * h + u : 2 * P * (h + 1) : 2], ident[:])
+            grouped = sbuf(name + "_grouped", I, BF16)
+            nc.scalar.copy(
+                grouped[:].bitcast(F32).rearrange("p (h m u) -> p h m u", h=PASSES, u=2),
+                turned[:].rearrange("p (h u m) -> p h m u", h=PASSES, u=2),
+            )
+            mx = mx_tiles(name, PASSES * P)
+            quantize(mx[0][:], mx[1][:], grouped[:])
+            return mx
+
+        def values(r):
+            val16 = sbuf("val16_%d" % r, I, BF16)
+            for h in range(PASSES):
+                nc.vector.tensor_copy(val16[:, PASS * h : PASS * (h + 1)], val_pool[r][:].indirect(pass_offsets(h)))
+            return turn(val16, "val%d" % (r % 2), "val%d" % r)
+
+        expd = [sbuf("expd%d" % b, I, F32) for b in range(QB)]
+        gated = [sbuf("gated%d" % b, I, F32) for b in range(QB)]
+        total = [sbuf("total%d" % b, 1, F32) for b in range(QB)]
+        inverse = [sbuf("inverse%d" % b, 1, F32) for b in range(QB)]
+        val_mx = [values(0)]
+        for b in range(QB):
+            nc.scalar.activation(expd[b][:], negated[b][:], ACT.Exp, bias=least[b][PASSES - 1][:], scale=-1.0)
+            nc.vector.scalar_tensor_tensor(
+                gated[b][:].rearrange("p (g j) -> p g j", j=BLOCK),
+                expd[b][:].rearrange("p (g j) -> p g j", j=BLOCK),
+                1.0,
+                gate[:, G * b : G * (b + 1)].unsqueeze(2).to_broadcast([P, G, BLOCK]),
+                ALU.mult,
+                ALU.mult,
+                accum_out=total[b][:],
+            )
+        val_mx.append(values(1))
+        weight_mx = []
+        for b in range(QB):
+            nc.vector.reciprocal(inverse[b][:], total[b][:])
+            weight16 = sbuf("weight16_%d" % b, I, BF16)
+            nc.vector.scalar_tensor_tensor(weight16[:], gated[b][:], inverse[b][:], size_all[:], ALU.mult, ALU.mult)
+            weight_mx.append(turn(weight16, "score%d" % b, "weight%d" % b))
+        val_mx.append(values(2))
+        val_mx.append(values(3))
+
+        result = sbuf("result", PACK * Q, F32)
+        result_view = result[:].rearrange("p (r q) -> p r q", r=PACK)
+        result16 = sbuf("result16", PACK * Q, BF16)
+        result_mx = mx_tiles("result", Q)
+        sums = [bank("score%d" % (QB + b), "sums%d" % b) for b in range(QB)]
+        for r in range(PACK):
+            for b in range(QB):
+                for h in range(PASSES):
+                    cols = slice(P * h, P * (h + 1))
+                    multiply(sums[b][:, P * r : P * (r + 1)], val_mx[r], cols, weight_mx[b], cols, h == 0, h == PASSES - 1)
+
+        def to_float32(b):
+            nc.scalar.copy(result_view[:, :, P * b : P * (b + 1)], sums[b][:].rearrange("p (r q) -> p r q", r=PACK))
+
+        def to_planes(b):
+            part = result16[:, PASS * b : PASS * (b + 1)]
+            nc.vector.tensor_copy(part.rearrange("p (q r) -> p q r", r=PACK), sums[b][:].rearrange("p (r q) -> p q r", r=PACK))
+
+        to_planes(0)
+        to_float32(1)
+        to_planes(1)
+        to_float32(0)
+        quantize(result_mx[0][:], result_mx[1][:], result16[:])
+        nc.scalar.dma_start(out_0.rearrange("(p r) q -> p (r q)", r=PACK), result[:])
+        nc.sync.dma_start(out_1.rearrange("z p c r -> p (z c r)").bitcast(I32), result_mx[0][:].bitcast(I32))
+        for quad in range(4):
+            nc.sync.dma_start(out_2[0, 4 * quad : 4 * quad + 4, :].bitcast(I32), result_mx[1][32 * quad : 32 * quad + 4, :].bitcast(I32))

@@ -15,16 +15,16 @@ U8 = mybir.dt.uint8
 FP8X4 = mybir.dt.float8_e4m3fn_x4
 ALU = mybir.AluOpType
 ACT = mybir.ActivationFunctionType
-AXIS = mybir.AxisListType
 
 P = 128
 PACK = 4
 PASS = P * PACK
-BLOCK = I // G
-RUN = I // P
-QB = Q // P
 PASSES = I // PASS
-LIST_COLS = PASS // 16
+BLOCK = I // G
+QB = Q // P
+SIZE_ROW = I // P
+RUN = I // P
+SCALAR_PLANE = 1
 
 
 def tile_attend_moba_pl_kernel(tc, query, keys, th, size, vals, offs, out_0, out_1, out_2):
@@ -33,16 +33,19 @@ def tile_attend_moba_pl_kernel(tc, query, keys, th, size, vals, offs, out_0, out
         sb = ctx.enter_context(tc.tile_pool(name="sb", bufs=1))
         ps = ctx.enter_context(tc.psum_pool(name="ps", bufs=1))
 
-        def sbuf(name, cols, dtype):
-            return sb.tile([P, cols], dtype, name=name, align_bytes=64)
+        def sbuf(name, cols, dtype, tag=None):
+            return sb.tile([P, cols], dtype, name=name, tag=tag or name, align_bytes=64)
 
         def bank(tag, name):
             return ps.tile([P, PASS], F32, name=name, tag=tag)
 
-        def quantize(codes, scales, values):
-            nc.vector.quantize_mx(out=codes.bitcast(FP8X4), scales=scales, in_=values)
+        def mx_tiles(name, cols, tag=None):
+            return sbuf(name + "_codes", cols, U32, tag), sbuf(name + "_scales", cols, U8)
 
-        def multiply(out, lhs, lhs_cols, rhs, rhs_cols, start, stop):
+        def quantize(mx, cols, values16):
+            nc.vector.quantize_mx(out=mx[0][:, cols].bitcast(FP8X4), scales=mx[1][:, cols], in_=values16)
+
+        def multiply(out, lhs, lhs_cols, rhs, rhs_cols, start=True, stop=True):
             nc.tensor.matmul_mx(
                 out=out,
                 lhsT=lhs[0][:, lhs_cols].bitcast(FP8X4),
@@ -53,59 +56,51 @@ def tile_attend_moba_pl_kernel(tc, query, keys, th, size, vals, offs, out_0, out
                 stop=stop,
             )
 
-        def mx_tiles(name, cols):
-            return sbuf(name + "_codes", cols, U32), sbuf(name + "_scales", cols, U8)
+        def span(width, n, count=1):
+            return slice(width * n, width * (n + count))
 
         offsets = sb.tile([P, I // 16], U16, name="offsets")
         nc.sync.dma_start(offsets[:], offs)
-        size_rows = sbuf("size_rows", RUN, F32)
-        nc.scalar.dma_start(size_rows[:], size.rearrange("o (n m) -> (o n) m", m=RUN))
+        size_rows = sbuf("size_rows", SIZE_ROW, F32)
+        nc.scalar.dma_start(size_rows[:], size.rearrange("o (n m) -> (o n) m", m=SIZE_ROW))
         th_cols = sbuf("th_cols", QB, F32)
-        with nc.allow_non_contiguous_dma(reason="one threshold a partition and query block"):
+        with nc.allow_non_contiguous_dma(reason="one threshold for each partition and group of query rows"):
             nc.scalar.dma_start(th_cols[:], th.rearrange("(b p) o -> p (b o)", p=P))
         ident = sbuf("ident", P, F32)
         make_identity(nc, ident[:])
-        key_rows = keys.rearrange("(p t) n -> p t n", t=PACK)
-        val_rows = vals.rearrange("(p t) n -> p t n", t=PACK)
         key_pool = [sbuf("key_pool%d" % t, T, F32) for t in range(PACK)]
-        val_pool = [sbuf("val_pool%d" % t, T, F32) for t in range(PACK)]
-        for t in range(PACK):
-            nc.sync.dma_start(key_pool[t][:], key_rows[:, t, :])
+        val_pool = [sbuf("val_pool%d" % r, T, F32) for r in range(PACK)]
         query_raw = sbuf("query_raw", PACK * Q, F32)
-        nc.sync.dma_start(val_pool[0][:], val_rows[:, 0, :])
+        key_planes = keys.rearrange("(p t) n -> p t n", t=PACK)
+        val_planes = vals.rearrange("(p r) n -> p r n", r=PACK)
+        for t in range(PACK):
+            nc.sync.dma_start(key_pool[t][:], key_planes[:, t, :])
         nc.sync.dma_start(query_raw[:], query.rearrange("(p t) q -> p (t q)", t=PACK))
-        for t in range(1, PACK):
-            nc.sync.dma_start(val_pool[t][:], val_rows[:, t, :])
+        for r in range(PACK):
+            nc.sync.dma_start(val_pool[r][:], val_planes[:, r, :])
+
+        def listed(pool, h):
+            return pool[:].indirect(offsets[:, span(PASS // 16, h)])
 
         size_all = sbuf("size_all", I, F32)
-        size_view = size_all[:].rearrange("p (n m) -> p n m", m=RUN)
-        for half in range(2):
+        size_view = size_all[:].rearrange("p (n m) -> p n m", m=SIZE_ROW)
+        for half in range(SIZE_ROW // PACK):
             spread = bank("score%d" % half, "spread%d" % half)
             for m in range(PACK):
-                col = PACK * half + m
-                nc.tensor.transpose(spread[:, P * m : P * (m + 1)], size_rows[:, col : col + 1].to_broadcast([P, P]), ident[:])
-            nc.scalar.activation(
-                size_view[:, :, PACK * half : PACK * (half + 1)],
-                spread[:].rearrange("p (m n) -> p n m", m=PACK),
-                ACT.Copy,
-            )
-
-        def pass_offsets(h):
-            return offsets[:, LIST_COLS * h : LIST_COLS * (h + 1)]
+                column = size_rows[:, span(1, PACK * half + m)].to_broadcast([P, P])
+                nc.tensor.transpose(spread[:, span(P, m)], column, ident[:])
+            nc.scalar.activation(size_view[:, :, span(PACK, half)], spread[:].rearrange("p (m n) -> p n m", m=PACK), ACT.Copy)
 
         picked = sbuf("picked", PACK * I, F32)
         picked_view = picked[:].rearrange("p (t s) -> p s t", t=PACK)
         key16 = sbuf("key16", PACK * I, BF16)
         key16_view = key16[:].rearrange("p (s t) -> p s t", t=PACK)
-        key_mx = mx_tiles("key", I)
-        run_sums = bank("runs", "run_sums")
-        run_means = sbuf("run_means", PASS, F32)
-        back = bank("back", "back")
+        run_sums = bank("blocks", "run_sums")
 
         def sum_runs(t):
             for j in range(RUN):
                 nc.tensor.matmul(
-                    run_sums[:, P * t : P * (t + 1)],
+                    run_sums[:, span(P, t)],
                     picked[:, I * t + j : I * (t + 1) : RUN],
                     ident[:],
                     start=(j == 0),
@@ -113,70 +108,79 @@ def tile_attend_moba_pl_kernel(tc, query, keys, th, size, vals, offs, out_0, out
                     is_transpose=True,
                 )
 
-        def turn_back(t0, t1):
-            nc.scalar.activation(run_means[:, P * t0 : P * t1], run_sums[:, P * t0 : P * t1], ACT.Copy, scale=1.0 / BLOCK)
-            for t in range(t0, t1):
-                nc.tensor.transpose(back[:, P * t : P * (t + 1)], run_means[:, P * t : P * (t + 1)], ident[:])
-
-        def round_keys(slots, u):
-            nc.scalar.copy(key16_view[:, slots, 2 * u : 2 * u + 2], picked_view[:, slots, 2 * u : 2 * u + 2])
+        def round_keys(pair, slots):
+            nc.scalar.copy(key16_view[:, slots, span(2, pair)], picked_view[:, slots, span(2, pair)])
 
         last = PACK - 1
         for t in range(last):
-            nc.vector.tensor_copy(picked[:, I * t : I * (t + 1)], key_pool[t][:].indirect(offsets[:]))
+            nc.vector.tensor_copy(picked[:, span(I, t)], key_pool[t][:].indirect(offsets[:]))
             sum_runs(t)
             if t == 1:
-                round_keys(slice(0, I), 0)
-        turn_back(0, last)
+                round_keys(0, slice(0, I))
         for h in range(PASSES):
-            slots = slice(PASS * h, PASS * (h + 1))
-            nc.vector.tensor_copy(picked[:, I * last + PASS * h : I * last + PASS * (h + 1)], key_pool[last][:].indirect(pass_offsets(h)))
-            round_keys(slots, 1)
+            nc.vector.tensor_copy(picked[:, span(PASS, PASSES * last + h)], listed(key_pool[last], h))
+            round_keys(1, span(PASS, h))
         sum_runs(last)
-        turn_back(last, PACK)
+
+        def turn(values16, turned, grouped, h0, count):
+            words = values16[:].bitcast(F32)
+            for h in range(h0, h0 + count):
+                for u in range(2):
+                    nc.tensor.transpose(turned[:, span(P, 2 * h + u)], words[:, 2 * P * h + u : 2 * P * (h + 1) : 2], ident[:])
+            nc.scalar.copy(
+                grouped[:, span(PASS, h0, count)].bitcast(F32).rearrange("p (h m u) -> p h m u", m=P, u=2),
+                turned[:, span(2 * P, h0, count)].rearrange("p (h u m) -> p h m u", m=P, u=2),
+            )
+
+        val16 = [sbuf("val16_%d" % r, I, BF16) for r in range(PACK)]
+        val_grouped = []
+        val_mx = [mx_tiles("val%d" % r, PASSES * P) for r in range(PACK)]
+
+        def gather(r):
+            if r == SCALAR_PLANE:
+                rounded = sbuf("rounded", T, BF16)
+                for half in range(2):
+                    nc.scalar.activation(rounded[:, span(T // 2, half)], val_pool[r][:, span(T // 2, half)], ACT.Copy)
+                for h in range(PASSES):
+                    nc.scalar.activation(val16[r][:, span(PASS, h)], listed(rounded, h), ACT.Copy)
+            else:
+                for h in range(PASSES):
+                    nc.vector.tensor_copy(val16[r][:, span(PASS, h)], listed(val_pool[r], h))
+
+        def turn_values(r, tag=None):
+            val_grouped.append(sbuf("val_grouped%d" % r, I, BF16, tag))
+            turn(val16[r], bank("val%d" % (r % 2), "val_turned%d" % r), val_grouped[r], 0, PASSES)
+
+        key_mx = [mx_tiles("key%d" % h, PASS) for h in range(PASSES)]
 
         query16 = sbuf("query16", PACK * Q, BF16)
-        nc.scalar.copy(query16[:].rearrange("p (q t) -> p q t", t=PACK), query_raw[:].rearrange("p (t q) -> p q t", t=PACK))
+        nc.vector.tensor_copy(query16[:].rearrange("p (q t) -> p q t", t=PACK), query_raw[:].rearrange("p (t q) -> p q t", t=PACK))
         query_mx = mx_tiles("query", Q)
-        quantize(query_mx[0][:], query_mx[1][:], query16[:])
+        quantize(query_mx, slice(0, Q), query16[:])
 
-        negated = [sbuf("negated%d" % b, I, F32) for b in range(QB)]
-        least = [[sbuf("least%d_%d" % (b, h), 1, F32) for h in range(PASSES)] for b in range(QB)]
-        for h in range(PASSES):
-            slots = slice(PASS * h, PASS * (h + 1))
-            quantize(key_mx[0][:, slots], key_mx[1][:, slots], key16[:, PACK * PASS * h : PACK * PASS * (h + 1)])
-            for b in range(QB):
-                score = bank("score%d" % (QB * h + b), "score%d_%d" % (b, h))
-                multiply(score[:], query_mx, slice(P * b, P * (b + 1)), key_mx, slots, True, True)
-                nc.vector.tensor_scalar(
-                    negated[b][:, slots],
-                    score[:],
-                    -1.0,
-                    None if h == 0 else least[b][h - 1][:],
-                    ALU.mult,
-                    ALU.min,
-                    accum_out=least[b][h][:],
-                )
-
+        run_means = sbuf("run_means", PASS, F32)
+        nc.scalar.activation(run_means[:], run_sums[:], ACT.Copy, scale=1.0 / BLOCK)
+        back = bank("back", "back")
+        for t in range(PACK):
+            nc.tensor.transpose(back[:, span(P, t)], run_means[:, span(P, t)], ident[:])
         mean16 = sbuf("mean16", PACK * G, BF16)
-        with nc.allow_low_precision(reason="float32 sum, rounded once for the quantiser"):
+        with nc.allow_low_precision(reason="the sum is float32 and is rounded once, for the quantiser"):
             nc.vector.tensor_reduce(
                 mean16[:].rearrange("p (g t) -> p g t", t=PACK),
-                back[:].rearrange("p (t g h) -> p g t h", t=PACK, h=2),
-                AXIS.X,
+                back[:].rearrange("p (t g j) -> p g t j", t=PACK, j=BLOCK // RUN),
+                mybir.AxisListType.X,
                 ALU.add,
             )
         mean_mx = mx_tiles("mean", G)
-        quantize(mean_mx[0][:], mean_mx[1][:], mean16[:])
-        block_score = bank("runs", "block_score")
+        quantize(mean_mx, slice(0, G), mean16[:])
+        block_score = bank("blocks", "block_score")
+        for b in range(QB):
+            multiply(block_score[:, span(G, b)], query_mx, span(P, b), mean_mx, slice(0, G))
         above = sbuf("above", QB * G, F32)
         dist = sbuf("dist", QB * G, F32)
         for b in range(QB):
-            multiply(block_score[:, G * b : G * (b + 1)], query_mx, slice(P * b, P * (b + 1)), mean_mx, slice(0, G), True, True)
-        for b in range(QB):
-            cols = slice(G * b, G * (b + 1))
-            nc.scalar.activation(above[:, cols], block_score[:, cols], ACT.Relu, bias=th_cols[:, b : b + 1], scale=-4.0)
-            nc.scalar.activation(dist[:, cols], block_score[:, cols], ACT.Abs, bias=th_cols[:, b : b + 1], scale=-4.0)
+            for out, func in ((above, ACT.Relu), (dist, ACT.Abs)):
+                nc.scalar.activation(out[:, span(G, b)], block_score[:, span(G, b)], func, bias=th_cols[:, span(1, b)], scale=-4.0)
         fall = sbuf("fall", QB * G, F32)
         rise = sbuf("rise", QB * G, F32)
         nc.scalar.activation(fall[:], above[:], ACT.Exp, scale=-1.0)
@@ -184,78 +188,76 @@ def tile_attend_moba_pl_kernel(tc, query, keys, th, size, vals, offs, out_0, out
         gate = sbuf("gate", QB * G, F32)
         nc.vector.scalar_tensor_tensor(gate[:], rise[:], 1.0, fall[:], ALU.add, ALU.mult)
 
-        def turn(values16, tag, name):
-            words = values16[:].bitcast(F32)
-            turned = bank(tag, name + "_turned")
-            for h in range(PASSES):
-                for u in range(2):
-                    c = 2 * h + u
-                    nc.tensor.transpose(turned[:, P * c : P * (c + 1)], words[:, 2 * P * h + u : 2 * P * (h + 1) : 2], ident[:])
-            grouped = sbuf(name + "_grouped", I, BF16)
-            nc.scalar.copy(
-                grouped[:].bitcast(F32).rearrange("p (h m u) -> p h m u", h=PASSES, u=2),
-                turned[:].rearrange("p (h u m) -> p h m u", h=PASSES, u=2),
-            )
-            mx = mx_tiles(name, PASSES * P)
-            quantize(mx[0][:], mx[1][:], grouped[:])
-            return mx
+        negated = [sbuf("negated%d" % b, I, F32) for b in range(QB)]
+        least = [[sbuf("least%d_%d" % (b, h), 1, F32) for h in range(PASSES)] for b in range(QB)]
+        for h in range(PASSES):
+            quantize(key_mx[h], slice(0, PASS), key16[:, span(PACK * PASS, h)])
+            for b in range(QB):
+                score = bank("score%d" % (QB * h + b), "score%d_%d" % (b, h))
+                multiply(score[:], query_mx, span(P, b), key_mx[h], slice(0, PASS))
+                so_far = least[b][h - 1][:] if h else None
+                nc.vector.tensor_scalar(negated[b][:, span(PASS, h)], score[:], -1.0, so_far, ALU.mult, ALU.min, accum_out=least[b][h][:])
 
-        def values(r):
-            val16 = sbuf("val16_%d" % r, I, BF16)
-            for h in range(PASSES):
-                nc.vector.tensor_copy(val16[:, PASS * h : PASS * (h + 1)], val_pool[r][:].indirect(pass_offsets(h)))
-            return turn(val16, "val%d" % (r % 2), "val%d" % r)
+        gather(0)
 
         expd = [sbuf("expd%d" % b, I, F32) for b in range(QB)]
         gated = [sbuf("gated%d" % b, I, F32) for b in range(QB)]
         total = [sbuf("total%d" % b, 1, F32) for b in range(QB)]
         inverse = [sbuf("inverse%d" % b, 1, F32) for b in range(QB)]
-        val_mx = [values(0)]
         for b in range(QB):
             nc.scalar.activation(expd[b][:], negated[b][:], ACT.Exp, bias=least[b][PASSES - 1][:], scale=-1.0)
+        turn_values(0, "negated1")
+        gather(1)
+        turn_values(1)
+        for b in range(QB):
             nc.vector.scalar_tensor_tensor(
                 gated[b][:].rearrange("p (g j) -> p g j", j=BLOCK),
                 expd[b][:].rearrange("p (g j) -> p g j", j=BLOCK),
                 1.0,
-                gate[:, G * b : G * (b + 1)].unsqueeze(2).to_broadcast([P, G, BLOCK]),
+                gate[:, span(G, b)].unsqueeze(2).to_broadcast([P, G, BLOCK]),
                 ALU.mult,
                 ALU.mult,
                 accum_out=total[b][:],
             )
-        val_mx.append(values(1))
-        weight_mx = []
-        for b in range(QB):
             nc.vector.reciprocal(inverse[b][:], total[b][:])
-            weight16 = sbuf("weight16_%d" % b, I, BF16)
-            nc.vector.scalar_tensor_tensor(weight16[:], gated[b][:], inverse[b][:], size_all[:], ALU.mult, ALU.mult)
-            weight_mx.append(turn(weight16, "score%d" % b, "weight%d" % b))
-        val_mx.append(values(2))
-        val_mx.append(values(3))
+        for r in range(2, PACK):
+            gather(r)
+            turn_values(r)
+
+        weight16 = [sbuf("weight16_%d" % b, I, BF16) for b in range(QB)]
+        weight_grouped = [sbuf("weight_grouped%d" % b, I, BF16) for b in range(QB)]
+        weight_mx = [mx_tiles("weight%d" % b, PASSES * P) for b in range(QB)]
+
+        for b in range(QB):
+            for h in range(PASSES):
+                slots = span(PASS, h)
+                nc.vector.scalar_tensor_tensor(weight16[b][:, slots], gated[b][:, slots], inverse[b][:], size_all[:, slots], ALU.mult, ALU.mult)
+                turn(weight16[b], bank(("blocks", "back")[h], "weight_turned%d_%d" % (b, h)), weight_grouped[b], h, 1)
+                quantize(weight_mx[b], span(P, h), weight_grouped[b][:, slots])
+        for r in range(PACK):
+            quantize(val_mx[r], slice(0, PASSES * P), val_grouped[r][:])
 
         result = sbuf("result", PACK * Q, F32)
         result_view = result[:].rearrange("p (r q) -> p r q", r=PACK)
         result16 = sbuf("result16", PACK * Q, BF16)
         result_mx = mx_tiles("result", Q)
-        sums = [bank("score%d" % (QB + b), "sums%d" % b) for b in range(QB)]
-        for r in range(PACK):
-            for b in range(QB):
-                for h in range(PASSES):
-                    cols = slice(P * h, P * (h + 1))
-                    multiply(sums[b][:, P * r : P * (r + 1)], val_mx[r], cols, weight_mx[b], cols, h == 0, h == PASSES - 1)
+        out_planes = out_0.rearrange("(p r) q -> p r q", r=PACK)
+        out_words = out_1.rearrange("z p c r -> p (z c r)").bitcast(I32)
 
-        def to_float32(b):
-            nc.scalar.copy(result_view[:, :, P * b : P * (b + 1)], sums[b][:].rearrange("p (r q) -> p r q", r=PACK))
-
-        def to_planes(b):
-            part = result16[:, PASS * b : PASS * (b + 1)]
-            nc.vector.tensor_copy(part.rearrange("p (q r) -> p q r", r=PACK), sums[b][:].rearrange("p (r q) -> p q r", r=PACK))
-
-        to_planes(0)
-        to_float32(1)
-        to_planes(1)
-        to_float32(0)
-        quantize(result_mx[0][:], result_mx[1][:], result16[:])
-        nc.scalar.dma_start(out_0.rearrange("(p r) q -> p (r q)", r=PACK), result[:])
-        nc.sync.dma_start(out_1.rearrange("z p c r -> p (z c r)").bitcast(I32), result_mx[0][:].bitcast(I32))
+        sums = [bank("score%d" % r, "sums%d" % r) for r in range(PACK)]
+        for b in range(QB):
+            rows = span(P, b)
+            for h in range(PASSES):
+                for r in range(PACK):
+                    multiply(sums[r][:, rows], val_mx[r], span(P, h), weight_mx[b], span(P, h), h == 0, h == PASSES - 1)
+            for r in range(PACK):
+                copy = nc.vector.tensor_copy if b == QB - 1 and r >= PACK // 2 else nc.scalar.copy
+                copy(result_view[:, r, rows], sums[r][:, rows])
+            nc.scalar.dma_start(out_planes[:, :, rows], result_view[:, :, rows])
+            part = result16[:, span(PASS, b)]
+            nc.vector.tensor_copy(part.rearrange("p (q r) -> p q r", r=PACK), result_view[:, :, rows].rearrange("p r q -> p q r"))
+            quantize(result_mx, rows, part)
+            nc.sync.dma_start(out_words[:, rows], result_mx[0][:, rows].bitcast(I32))
         for quad in range(4):
-            nc.sync.dma_start(out_2[0, 4 * quad : 4 * quad + 4, :].bitcast(I32), result_mx[1][32 * quad : 32 * quad + 4, :].bitcast(I32))
+            queue = nc.sync if quad % 2 == 0 else nc.scalar
+            queue.dma_start(out_2[0, span(4, quad), :].bitcast(I32), result_mx[1][32 * quad : 32 * quad + 4, :].bitcast(I32))

from contextlib import ExitStack

import concourse.mybir as mybir
from concourse.masks import make_identity

D, T, I, Q, E, G = 512, 2048, 1024, 256, 512, 64
FLOPS = 2 * D * Q * G + 2 * D * Q * I + 2 * I * E * Q

F32 = mybir.dt.float32
BF16 = mybir.dt.bfloat16
I32 = mybir.dt.int32
U32 = mybir.dt.uint32
U16 = mybir.dt.uint16
U8 = mybir.dt.uint8
FP8X4 = mybir.dt.float8_e4m3fn_x4
ALU = mybir.AluOpType
ACT = mybir.ActivationFunctionType

P = 128
PACK = 4
PASS = P * PACK
PASSES = I // PASS
BLOCK = I // G
QB = Q // P
SIZE_ROW = I // P
RUN = I // P
SCALAR_PLANE = 1


def tile_attend_moba_pl_kernel(tc, query, keys, th, size, vals, offs, out_0, out_1, out_2):
    nc = tc.nc
    with ExitStack() as ctx:
        sb = ctx.enter_context(tc.tile_pool(name="sb", bufs=1))
        ps = ctx.enter_context(tc.psum_pool(name="ps", bufs=1))

        def sbuf(name, cols, dtype, tag=None):
            return sb.tile([P, cols], dtype, name=name, tag=tag or name, align_bytes=64)

        def bank(tag, name):
            return ps.tile([P, PASS], F32, name=name, tag=tag)

        def mx_tiles(name, cols, tag=None):
            return sbuf(name + "_codes", cols, U32, tag), sbuf(name + "_scales", cols, U8)

        def quantize(mx, cols, values16):
            nc.vector.quantize_mx(out=mx[0][:, cols].bitcast(FP8X4), scales=mx[1][:, cols], in_=values16)

        def multiply(out, lhs, lhs_cols, rhs, rhs_cols, start=True, stop=True):
            nc.tensor.matmul_mx(
                out=out,
                lhsT=lhs[0][:, lhs_cols].bitcast(FP8X4),
                lhsT_scale=lhs[1][:, lhs_cols],
                rhs=rhs[0][:, rhs_cols].bitcast(FP8X4),
                rhs_scale=rhs[1][:, rhs_cols],
                start=start,
                stop=stop,
            )

        def span(width, n, count=1):
            return slice(width * n, width * (n + count))

        offsets = sb.tile([P, I // 16], U16, name="offsets")
        nc.sync.dma_start(offsets[:], offs)
        size_rows = sbuf("size_rows", SIZE_ROW, F32)
        nc.scalar.dma_start(size_rows[:], size.rearrange("o (n m) -> (o n) m", m=SIZE_ROW))
        th_cols = sbuf("th_cols", QB, F32)
        with nc.allow_non_contiguous_dma(reason="one threshold for each partition and group of query rows"):
            nc.scalar.dma_start(th_cols[:], th.rearrange("(b p) o -> p (b o)", p=P))
        ident = sbuf("ident", P, F32)
        make_identity(nc, ident[:])
        key_pool = [sbuf("key_pool%d" % t, T, F32) for t in range(PACK)]
        val_pool = [sbuf("val_pool%d" % r, T, F32) for r in range(PACK)]
        query_raw = sbuf("query_raw", PACK * Q, F32)
        key_planes = keys.rearrange("(p t) n -> p t n", t=PACK)
        val_planes = vals.rearrange("(p r) n -> p r n", r=PACK)
        for t in range(PACK):
            nc.sync.dma_start(key_pool[t][:], key_planes[:, t, :])
        nc.sync.dma_start(query_raw[:], query.rearrange("(p t) q -> p (t q)", t=PACK))
        for r in range(PACK):
            nc.sync.dma_start(val_pool[r][:], val_planes[:, r, :])

        def listed(pool, h):
            return pool[:].indirect(offsets[:, span(PASS // 16, h)])

        size_all = sbuf("size_all", I, F32)
        size_view = size_all[:].rearrange("p (n m) -> p n m", m=SIZE_ROW)
        for half in range(SIZE_ROW // PACK):
            spread = bank("score%d" % half, "spread%d" % half)
            for m in range(PACK):
                column = size_rows[:, span(1, PACK * half + m)].to_broadcast([P, P])
                nc.tensor.transpose(spread[:, span(P, m)], column, ident[:])
            nc.scalar.activation(size_view[:, :, span(PACK, half)], spread[:].rearrange("p (m n) -> p n m", m=PACK), ACT.Copy)

        picked = sbuf("picked", PACK * I, F32)
        picked_view = picked[:].rearrange("p (t s) -> p s t", t=PACK)
        key16 = sbuf("key16", PACK * I, BF16)
        key16_view = key16[:].rearrange("p (s t) -> p s t", t=PACK)
        run_sums = bank("blocks", "run_sums")

        def sum_runs(t):
            for j in range(RUN):
                nc.tensor.matmul(
                    run_sums[:, span(P, t)],
                    picked[:, I * t + j : I * (t + 1) : RUN],
                    ident[:],
                    start=(j == 0),
                    stop=(j == RUN - 1),
                    is_transpose=True,
                )

        def round_keys(pair, slots):
            nc.scalar.copy(key16_view[:, slots, span(2, pair)], picked_view[:, slots, span(2, pair)])

        last = PACK - 1
        for t in range(last):
            nc.vector.tensor_copy(picked[:, span(I, t)], key_pool[t][:].indirect(offsets[:]))
            sum_runs(t)
            if t == 1:
                round_keys(0, slice(0, I))
        for h in range(PASSES):
            nc.vector.tensor_copy(picked[:, span(PASS, PASSES * last + h)], listed(key_pool[last], h))
            round_keys(1, span(PASS, h))
        sum_runs(last)

        def turn(values16, turned, grouped, h0, count):
            words = values16[:].bitcast(F32)
            for h in range(h0, h0 + count):
                for u in range(2):
                    nc.tensor.transpose(turned[:, span(P, 2 * h + u)], words[:, 2 * P * h + u : 2 * P * (h + 1) : 2], ident[:])
            nc.scalar.copy(
                grouped[:, span(PASS, h0, count)].bitcast(F32).rearrange("p (h m u) -> p h m u", m=P, u=2),
                turned[:, span(2 * P, h0, count)].rearrange("p (h u m) -> p h m u", m=P, u=2),
            )

        val16 = [sbuf("val16_%d" % r, I, BF16) for r in range(PACK)]
        val_grouped = []
        val_mx = [mx_tiles("val%d" % r, PASSES * P) for r in range(PACK)]

        def gather(r):
            if r == SCALAR_PLANE:
                rounded = sbuf("rounded", T, BF16)
                for half in range(2):
                    nc.scalar.activation(rounded[:, span(T // 2, half)], val_pool[r][:, span(T // 2, half)], ACT.Copy)
                for h in range(PASSES):
                    nc.scalar.activation(val16[r][:, span(PASS, h)], listed(rounded, h), ACT.Copy)
            else:
                for h in range(PASSES):
                    nc.vector.tensor_copy(val16[r][:, span(PASS, h)], listed(val_pool[r], h))

        def turn_values(r, tag=None):
            val_grouped.append(sbuf("val_grouped%d" % r, I, BF16, tag))
            turn(val16[r], bank("val%d" % (r % 2), "val_turned%d" % r), val_grouped[r], 0, PASSES)

        key_mx = [mx_tiles("key%d" % h, PASS) for h in range(PASSES)]

        query16 = sbuf("query16", PACK * Q, BF16)
        nc.vector.tensor_copy(query16[:].rearrange("p (q t) -> p q t", t=PACK), query_raw[:].rearrange("p (t q) -> p q t", t=PACK))
        query_mx = mx_tiles("query", Q)
        quantize(query_mx, slice(0, Q), query16[:])

        run_means = sbuf("run_means", PASS, F32)
        nc.scalar.activation(run_means[:], run_sums[:], ACT.Copy, scale=1.0 / BLOCK)
        back = bank("back", "back")
        for t in range(PACK):
            nc.tensor.transpose(back[:, span(P, t)], run_means[:, span(P, t)], ident[:])
        mean16 = sbuf("mean16", PACK * G, BF16)
        with nc.allow_low_precision(reason="the sum is float32 and is rounded once, for the quantiser"):
            nc.vector.tensor_reduce(
                mean16[:].rearrange("p (g t) -> p g t", t=PACK),
                back[:].rearrange("p (t g j) -> p g t j", t=PACK, j=BLOCK // RUN),
                mybir.AxisListType.X,
                ALU.add,
            )
        mean_mx = mx_tiles("mean", G)
        quantize(mean_mx, slice(0, G), mean16[:])
        block_score = bank("blocks", "block_score")
        for b in range(QB):
            multiply(block_score[:, span(G, b)], query_mx, span(P, b), mean_mx, slice(0, G))
        above = sbuf("above", QB * G, F32)
        dist = sbuf("dist", QB * G, F32)
        for b in range(QB):
            for out, func in ((above, ACT.Relu), (dist, ACT.Abs)):
                nc.scalar.activation(out[:, span(G, b)], block_score[:, span(G, b)], func, bias=th_cols[:, span(1, b)], scale=-4.0)
        fall = sbuf("fall", QB * G, F32)
        rise = sbuf("rise", QB * G, F32)
        nc.scalar.activation(fall[:], above[:], ACT.Exp, scale=-1.0)
        nc.scalar.activation(rise[:], dist[:], ACT.Tanh, scale=0.5)
        gate = sbuf("gate", QB * G, F32)
        nc.vector.scalar_tensor_tensor(gate[:], rise[:], 1.0, fall[:], ALU.add, ALU.mult)

        negated = [sbuf("negated%d" % b, I, F32) for b in range(QB)]
        least = [[sbuf("least%d_%d" % (b, h), 1, F32) for h in range(PASSES)] for b in range(QB)]
        for h in range(PASSES):
            quantize(key_mx[h], slice(0, PASS), key16[:, span(PACK * PASS, h)])
            for b in range(QB):
                score = bank("score%d" % (QB * h + b), "score%d_%d" % (b, h))
                multiply(score[:], query_mx, span(P, b), key_mx[h], slice(0, PASS))
                so_far = least[b][h - 1][:] if h else None
                nc.vector.tensor_scalar(negated[b][:, span(PASS, h)], score[:], -1.0, so_far, ALU.mult, ALU.min, accum_out=least[b][h][:])

        gather(0)

        expd = [sbuf("expd%d" % b, I, F32) for b in range(QB)]
        gated = [sbuf("gated%d" % b, I, F32) for b in range(QB)]
        total = [sbuf("total%d" % b, 1, F32) for b in range(QB)]
        inverse = [sbuf("inverse%d" % b, 1, F32) for b in range(QB)]
        for b in range(QB):
            nc.scalar.activation(expd[b][:], negated[b][:], ACT.Exp, bias=least[b][PASSES - 1][:], scale=-1.0)
        turn_values(0, "negated1")
        gather(1)
        turn_values(1)
        for b in range(QB):
            nc.vector.scalar_tensor_tensor(
                gated[b][:].rearrange("p (g j) -> p g j", j=BLOCK),
                expd[b][:].rearrange("p (g j) -> p g j", j=BLOCK),
                1.0,
                gate[:, span(G, b)].unsqueeze(2).to_broadcast([P, G, BLOCK]),
                ALU.mult,
                ALU.mult,
                accum_out=total[b][:],
            )
            nc.vector.reciprocal(inverse[b][:], total[b][:])
        for r in range(2, PACK):
            gather(r)
            turn_values(r)

        weight16 = [sbuf("weight16_%d" % b, I, BF16) for b in range(QB)]
        weight_grouped = [sbuf("weight_grouped%d" % b, I, BF16) for b in range(QB)]
        weight_mx = [mx_tiles("weight%d" % b, PASSES * P) for b in range(QB)]

        for b in range(QB):
            for h in range(PASSES):
                slots = span(PASS, h)
                nc.vector.scalar_tensor_tensor(weight16[b][:, slots], gated[b][:, slots], inverse[b][:], size_all[:, slots], ALU.mult, ALU.mult)
                turn(weight16[b], bank(("blocks", "back")[h], "weight_turned%d_%d" % (b, h)), weight_grouped[b], h, 1)
                quantize(weight_mx[b], span(P, h), weight_grouped[b][:, slots])
        for r in range(PACK):
            quantize(val_mx[r], slice(0, PASSES * P), val_grouped[r][:])

        result = sbuf("result", PACK * Q, F32)
        result_view = result[:].rearrange("p (r q) -> p r q", r=PACK)
        result16 = sbuf("result16", PACK * Q, BF16)
        result_mx = mx_tiles("result", Q)
        out_planes = out_0.rearrange("(p r) q -> p r q", r=PACK)
        out_words = out_1.rearrange("z p c r -> p (z c r)").bitcast(I32)

        sums = [bank("score%d" % r, "sums%d" % r) for r in range(PACK)]
        for b in range(QB):
            rows = span(P, b)
            for h in range(PASSES):
                for r in range(PACK):
                    multiply(sums[r][:, rows], val_mx[r], span(P, h), weight_mx[b], span(P, h), h == 0, h == PASSES - 1)
            for r in range(PACK):
                copy = nc.vector.tensor_copy if b == QB - 1 and r >= PACK // 2 else nc.scalar.copy
                copy(result_view[:, r, rows], sums[r][:, rows])
            nc.scalar.dma_start(out_planes[:, :, rows], result_view[:, :, rows])
            part = result16[:, span(PASS, b)]
            nc.vector.tensor_copy(part.rearrange("p (q r) -> p q r", r=PACK), result_view[:, :, rows].rearrange("p r q -> p q r"))
            quantize(result_mx, rows, part)
            nc.sync.dma_start(out_words[:, rows], result_mx[0][:, rows].bitcast(I32))
        for quad in range(4):
            queue = nc.sync if quad % 2 == 0 else nc.scalar
            queue.dma_start(out_2[0, span(4, quad), :].bitcast(I32), result_mx[1][32 * quad : 32 * quad + 4, :].bitcast(I32))
